import numpy as np
import ml_dtypes


def mxq(x, axis, fmt="e4m3"):
    dtype, down = {"e4m3": (ml_dtypes.float8_e4m3fn, 7), "e5m2": (ml_dtypes.float8_e5m2, 14)}[fmt]
    v = np.moveaxis(np.asarray(x, np.float32).astype(ml_dtypes.bfloat16).astype(np.float64), axis, -1)
    blocks = v.reshape(v.shape[:-1] + (-1, 32))
    amax = np.abs(blocks).max(-1, keepdims=True)
    byte = np.maximum(np.where(amax > 0, np.frexp(amax)[1] - 1 + 127, 0) - down, 1)
    scale = np.exp2(byte - 127.0)
    codes = (blocks / scale).astype(np.float32).astype(dtype).astype(np.float64)
    return np.moveaxis((codes * scale).reshape(v.shape), -1, axis)


WIDE = False


def mx_kscale(k):
    if not WIDE:
        return np.ones(k)
    levels = np.array([10, -10, 5, -5, 0])
    if k % 512:
        return np.exp2(np.random.permutation(np.resize(levels, k // 32))).repeat(32)
    a = np.empty((k // 512, 16))
    for p in range(k // 512):
        a[p, :8] = np.random.permutation(np.resize(levels, 8))
        for g in range(8):
            far = levels[np.abs(levels - a[p, g]) >= 10]
            a[p, g + 8] = far[np.random.randint(len(far))]
    return np.exp2(a.ravel()).repeat(32)


def f64(x):
    return np.asarray(x).astype(np.float64)


def striped(idx):
    return np.tile(idx.reshape(-1, 16).T, (8, 1)).astype(np.uint16)


def unstriped(offs):
    return offs[:16].T.reshape(-1).astype(np.int64)


def striped8(idx):
    return np.concatenate([x.reshape(-1, 16).T for x in idx]).astype(np.uint16)


def runs(offs, k):
    lists = np.stack([offs[16 * r : 16 * r + 16].T.reshape(-1) for r in range(8)]).astype(np.int64)
    return lists[np.arange(k) % 512 // 64]


def pack_weight(w):
    k, n = w.shape
    w = f64(np.asarray(w, np.float32).astype(ml_dtypes.bfloat16)).reshape(k // 32, 32, n)
    amax = np.abs(w).max(1)
    byte = np.clip(np.where(amax > 0, np.frexp(amax)[1] - 1 + 127 - 7, 1), 1, 254)
    scaled = (w * np.exp2(127.0 - byte)[:, None, :]).reshape(k, n).astype(np.float32)
    words = np.ascontiguousarray(scaled.reshape(k // 512, 128, 4, n).transpose(0, 1, 3, 2)).astype(ml_dtypes.float8_e4m3fn).view(np.uint8)
    return words, np.ascontiguousarray(byte.astype(np.uint8).reshape(k // 512, 16, n))


def unpack_weight(words, scales):
    g, p, n, _ = words.shape
    vals = np.ascontiguousarray(words).view(ml_dtypes.float8_e4m3fn).astype(np.float64) * np.repeat(np.exp2(scales.astype(np.float64) - 127.0), 8, axis=1)[..., None]
    return vals.transpose(0, 1, 3, 2).reshape(g * 512, n)


K, T, S, N, H = 512, 2048, 512, 512, 512


def setup_inputs():
    n = np.random.standard_normal
    s = mx_kscale(K)[:, None]
    u = mx_kscale(S)
    packed_xT = pack_weight(n((K, T)) * s)
    return {
        "x_words": packed_xT[0],
        "x_scales": packed_xT[1],
        "wa": (n((K, H)) / np.sqrt(K) / s).astype(np.float32),
        "wb": (n((K, N)) / np.sqrt(K) / s).astype(np.float32),
        "gt": (np.random.uniform(0.5, 1.5, (S, 1)) * u[:, None]).astype(np.float32),
        "gi": (np.random.uniform(0.5, 1.5, (S, 1)) / u[:, None]).astype(np.float32),
        "offs": striped(np.random.permutation(T)[:S]),
        "two": striped(np.random.permutation(T)[:S]),
        "fl": striped8(np.stack([np.random.permutation(N) for _ in range(8)])),
    }


def reference(x_words, x_scales, wa, wb, gt, gi, offs, two, fl):
    xq = unpack_weight(x_words, x_scales)[:, unstriped(offs)]
    a = xq.T @ mxq(f64(wa), 0, "e4m3")
    z = f64(gt) * a
    zq = mxq(z, 0, "e4m3")
    x_two = unpack_weight(x_words, x_scales)[:, unstriped(two)]
    b = x_two.T @ mxq(f64(wb), 0, "e4m3")
    z2 = f64(gi) * b
    d = b[np.arange(S)[:, None], runs(fl, S)]
    z3 = f64(gi) * d
    m1 = 0.03125 * ((zq.T @ mxq(z2, 0, "e4m3")) - ((zq.T @ mxq(z3, 0, "e4m3"))))
    return (m1) ** 2

@@ -1,0 +1,190 @@
+from contextlib import ExitStack
+
+import concourse.mybir as mybir
+from concourse.masks import make_identity
+
+K, T, S, N, H = 512, 2048, 512, 512, 512
+FLOPS = 4 * 2 * 512 * 512 * 512
+
+F32 = mybir.dt.float32
+BF16 = mybir.dt.bfloat16
+I32 = mybir.dt.int32
+U32 = mybir.dt.uint32
+U16 = mybir.dt.uint16
+U8 = mybir.dt.uint8
+FP8X4 = mybir.dt.float8_e4m3fn_x4
+ACT = mybir.ActivationFunctionType
+ALU = mybir.AluOpType
+
+P = 128
+PACK = 4
+RUN = 8
+HALF = 256
+LINE = 4
+
+
+def side_by_side(grouped):
+    return grouped.rearrange("p (c i) t -> p c t i", i=LINE)
+
+
+def by_rows(rows):
+    return rows.rearrange("p t (c i) -> p c t i", i=LINE)
+
+
+def quantize(nc, codes, scales, grouped):
+    nc.vector.quantize_mx(out=codes.bitcast(FP8X4), scales=scales, in_=grouped.rearrange("p c t -> p (c t)"))
+
+
+def tile_picked_momdiff_square_p_kernel(tc, x_words, x_scales, wa, wb, gt, gi, offs, two, fl, out):
+    nc = tc.nc
+    with ExitStack() as ctx:
+        sb = ctx.enter_context(tc.tile_pool(name="sb", bufs=1))
+        ps = ctx.enter_context(tc.psum_pool(name="ps", bufs=1))
+
+        def bank(b, shape):
+            return ps.tile(shape, F32, name="bank%d" % b, tag="bank%d" % b)
+
+        scale_table = sb.tile([P, T], U8, name="scale_table", align_bytes=64)
+        nc.vector.memset(scale_table[:].bitcast(I32), 0)
+        two_sb = sb.tile([P, S // 16], U16, name="two_sb")
+        offs_sb = sb.tile([P, S // 16], U16, name="offs_sb")
+        fl_sb = sb.tile([P, N // 16], U16, name="fl_sb")
+        nc.sync.dma_start(two_sb[:], two)
+        nc.sync.dma_start(offs_sb[:], offs)
+        for q in range(4):
+            nc.sync.dma_start(scale_table[32 * q : 32 * q + 4, :].bitcast(I32), x_scales[0, 4 * q : 4 * q + 4, :].bitcast(I32))
+        word_table = sb.tile([P, T], I32, name="word_table", align_bytes=64)
+        nc.sync.dma_start(word_table[:], x_words[0].rearrange("p c r -> p (c r)").bitcast(I32))
+
+        def load_weight_half(w, h, name):
+            raw = sb.tile([P, PACK, HALF], F32, name=name)
+            nc.sync.dma_start(raw[:], w.rearrange("(p j) n -> p j n", j=PACK)[:, :, h * HALF : (h + 1) * HALF])
+            return raw
+
+        wb_raw = [load_weight_half(wb, h, "wb_raw%d" % h) for h in range(2)]
+
+        g_rows = sb.tile([P, P], F32, name="g_rows")
+        nc.gpsimd.memset(g_rows[:], 0.0)
+        for first, g in ((0, gi), (PACK, gt)):
+            nc.sync.dma_start(
+                g_rows[first : first + PACK, :].rearrange("t (b e) -> t b e", e=RUN),
+                g.rearrange("(b t e) o -> t b (e o)", t=PACK, e=RUN),
+            )
+        nc.sync.dma_start(fl_sb[:], fl)
+        wa_raw = [load_weight_half(wa, h, "wa_raw%d" % h) for h in range(2)]
+        ident = sb.tile([P, P], F32, name="ident")
+        make_identity(nc, ident[:])
+        g_turned = bank(7, [P, P])
+        nc.tensor.transpose(g_turned[:], g_rows[:], ident[:])
+        g_cols = sb.tile([P, 2 * PACK], F32, name="g_cols")
+        nc.scalar.copy(g_cols[:], g_turned[:, : 2 * PACK])
+
+        def pick_scales(offsets, name):
+            picked = sb.tile([P, S], U8, name=name + "_picked", align_bytes=64)
+            nc.vector.tensor_copy(picked[:], scale_table[:].indirect(offsets[:]))
+            dealt = sb.tile([P, PACK * P], U8, name=name, align_bytes=64)
+            nc.vector.tensor_copy(
+                dealt[:].bitcast(I32).rearrange("p (t b e) -> p b t e", t=PACK, e=RUN // 4),
+                picked[:].bitcast(I32).rearrange("p (b t e) -> p b t e", t=PACK, e=RUN // 4),
+            )
+            return dealt
+
+        def pick_words(offsets, name, tag):
+            dealt = sb.tile([P, PACK * P], U32, name=name, tag=tag, align_bytes=64)
+            nc.vector.tensor_copy(
+                dealt[:].rearrange("p (t b e) -> p b t e", t=PACK, e=RUN),
+                word_table[:].bitcast(U32).indirect(offsets[:]),
+            )
+            return dealt
+
+        def quantize_weight_half(raw, name, tag):
+            grouped = sb.tile([P, HALF, PACK], BF16, name=name + "_grouped", tag=tag, align_bytes=64)
+            nc.scalar.copy(side_by_side(grouped[:]), by_rows(raw[:]))
+            codes = sb.tile([P, HALF], U32, name=name + "_codes", tag=name + "_codes", align_bytes=64)
+            scales = sb.tile([P, HALF], U8, name=name + "_scales", align_bytes=64)
+            quantize(nc, codes[:], scales[:], grouped[:])
+            return codes, scales
+
+        xb_scales = pick_scales(two_sb, "xb_scales")
+        xa_scales = pick_scales(offs_sb, "xa_scales")
+        xb_words = pick_words(two_sb, "xb_words", "xb_words")
+
+        wbq = [quantize_weight_half(wb_raw[h], "wb%d" % h, "wb%d_grouped" % h) for h in range(2)]
+        window = [sb.tile([P, N], F32, name="window%d" % t) for t in range(PACK)]
+        for h in range(2):
+            codes, scales = wbq[h]
+            for t in range(PACK):
+                rows = slice(t * P, (t + 1) * P)
+                b_ps = bank(PACK * h + t, [P, HALF])
+                nc.tensor.matmul_mx(
+                    out=b_ps[:], lhsT=xb_words[:, rows].bitcast(FP8X4), lhsT_scale=xb_scales[:, rows],
+                    rhs=codes[:].bitcast(FP8X4), rhs_scale=scales[:], start=True, stop=True,
+                )
+                nc.scalar.activation(window[t][:, h * HALF : (h + 1) * HALF], b_ps[:], ACT.Copy, scale=g_cols[:, t : t + 1])
+
+        xa_words = pick_words(offs_sb, "xa_words", "xa_words")
+
+        z2_rows = sb.tile([P, PACK, N], F32, name="z2_rows")
+        for t in range(PACK):
+            nc.sync.dma_start(z2_rows[:, t, :], window[t][:])
+
+        z3_rows = [sb.tile([P, PACK, HALF], BF16, name="z3_rows%d" % h) for h in range(2)]
+        for h in range(2):
+            for t in range(PACK):
+                nc.vector.tensor_copy(z3_rows[h][:, t, :], window[t][:].indirect(fl_sb[:, 16 * h : 16 * (h + 1)]))
+
+        waq = [quantize_weight_half(wa_raw[h], "wa%d" % h, ("xb_words", "wb1_codes")[h]) for h in range(2)]
+
+        zq = []
+        for h in range(2):
+            codes, scales = waq[h]
+            grouped = sb.tile([P, HALF, PACK], BF16, name="z_grouped%d" % h, align_bytes=64)
+            for u in range(2):
+                cols = slice(u * P, (u + 1) * P)
+                a_ps = bank(2 * h + u, [P, PACK, P])
+                for t in range(PACK):
+                    rows = slice(t * P, (t + 1) * P)
+                    nc.tensor.matmul_mx(
+                        out=a_ps[:, t, :], lhsT=xa_words[:, rows].bitcast(FP8X4), lhsT_scale=xa_scales[:, rows],
+                        rhs=codes[:, cols].bitcast(FP8X4), rhs_scale=scales[:, cols], start=True, stop=True,
+                    )
+                nc.vector.tensor_tensor(
+                    grouped[:, cols, :], a_ps[:].rearrange("p t c -> p c t"),
+                    g_cols[:, PACK:].unsqueeze(1).to_broadcast([P, P, PACK]), ALU.mult,
+                )
+            z_codes = sb.tile([P, HALF], U32, name="z_codes%d" % h, align_bytes=64)
+            z_scales = sb.tile([P, HALF], U8, name="z_scales%d" % h, align_bytes=64)
+            quantize(nc, z_codes[:], z_scales[:], grouped[:])
+            zq.append((z_codes, z_scales))
+
+        def quantized(grouped, name):
+            codes = sb.tile([P, HALF], U32, name=name + "_codes", align_bytes=64)
+            scales = sb.tile([P, HALF], U8, name=name + "_scales", align_bytes=64)
+            quantize(nc, codes[:], scales[:], grouped[:])
+            return codes, scales
+
+        def z2_half(h):
+            grouped = sb.tile([P, HALF, PACK], BF16, name="z2_grouped%d" % h, align_bytes=64)
+            nc.scalar.activation(side_by_side(grouped[:]), by_rows(z2_rows[:, :, h * HALF : (h + 1) * HALF]), ACT.Copy, scale=-1.0)
+            return quantized(grouped, "z2_%d" % h)
+
+        def z3_half(h):
+            grouped = sb.tile([P, HALF, PACK], BF16, name="z3_grouped%d" % h, align_bytes=64)
+            nc.scalar.copy(side_by_side(grouped[:]), by_rows(z3_rows[h][:]))
+            return quantized(grouped, "z3_%d" % h)
+
+        moving = [(z3_half(0), z2_half(0)), (z2_half(1), z3_half(1))]
+        for h in range(2):
+            m_ps = [bank(PACK * (1 - h) + m, [P, HALF]) for m in range(H // P)]
+            for step, (codes, scales) in enumerate(moving[h]):
+                for m in range(H // P):
+                    z_codes, z_scales = zq[m // 2]
+                    rows = slice((m % 2) * P, (m % 2 + 1) * P)
+                    nc.tensor.matmul_mx(
+                        out=m_ps[m][:], lhsT=z_codes[:, rows].bitcast(FP8X4), lhsT_scale=z_scales[:, rows],
+                        rhs=codes[:].bitcast(FP8X4), rhs_scale=scales[:], start=step == 0, stop=step == 1,
+                    )
+            for m in range(H // P):
+                result = sb.tile([P, HALF], F32, name="result%d_%d" % (h, m))
+                nc.scalar.activation(result[:], m_ps[m][:], ACT.Square, scale=0.03125)
+                nc.sync.dma_start(out[m * P : (m + 1) * P, h * HALF : (h + 1) * HALF], result[:])

@@ -45,14 +45,14 @@ def tile_picked_momdiff_square_p_kernel(tc, x_words, x_scales, wa, wb, gt, gi, o
             return ps.tile(shape, F32, name="bank%d" % b, tag="bank%d" % b)
 
         scale_table = sb.tile([P, T], U8, name="scale_table", align_bytes=64)
-        nc.vector.memset(scale_table[:].bitcast(I32), 0)
+        nc.gpsimd.memset(scale_table[:].bitcast(I32), 0)
         two_sb = sb.tile([P, S // 16], U16, name="two_sb")
         offs_sb = sb.tile([P, S // 16], U16, name="offs_sb")
         fl_sb = sb.tile([P, N // 16], U16, name="fl_sb")
         nc.sync.dma_start(two_sb[:], two)
-        nc.sync.dma_start(offs_sb[:], offs)
         for q in range(4):
-            nc.sync.dma_start(scale_table[32 * q : 32 * q + 4, :].bitcast(I32), x_scales[0, 4 * q : 4 * q + 4, :].bitcast(I32))
+            (nc.scalar, nc.sync)[q % 2].dma_start(scale_table[32 * q : 32 * q + 4, :].bitcast(I32), x_scales[0, 4 * q : 4 * q + 4, :].bitcast(I32))
+        nc.sync.dma_start(offs_sb[:], offs)
         word_table = sb.tile([P, T], I32, name="word_table", align_bytes=64)
         nc.sync.dma_start(word_table[:], x_words[0].rearrange("p c r -> p (c r)").bitcast(I32))
 
@@ -61,8 +61,6 @@ def tile_picked_momdiff_square_p_kernel(tc, x_words, x_scales, wa, wb, gt, gi, o
             nc.sync.dma_start(raw[:], w.rearrange("(p j) n -> p j n", j=PACK)[:, :, h * HALF : (h + 1) * HALF])
             return raw
 
-        wb_raw = [load_weight_half(wb, h, "wb_raw%d" % h) for h in range(2)]
-
         g_rows = sb.tile([P, P], F32, name="g_rows")
         nc.gpsimd.memset(g_rows[:], 0.0)
         for first, g in ((0, gi), (PACK, gt)):
@@ -70,24 +68,18 @@ def tile_picked_momdiff_square_p_kernel(tc, x_words, x_scales, wa, wb, gt, gi, o
                 g_rows[first : first + PACK, :].rearrange("t (b e) -> t b e", e=RUN),
                 g.rearrange("(b t e) o -> t b (e o)", t=PACK, e=RUN),
             )
+        wa_raw = [load_weight_half(wa, 0, "wa_raw0")]
+        wb_raw = [load_weight_half(wb, h, "wb_raw%d" % h) for h in range(2)]
         nc.sync.dma_start(fl_sb[:], fl)
-        wa_raw = [load_weight_half(wa, h, "wa_raw%d" % h) for h in range(2)]
+        wa_raw.append(load_weight_half(wa, 1, "wa_raw1"))
         ident = sb.tile([P, P], F32, name="ident")
         make_identity(nc, ident[:])
         g_turned = bank(7, [P, P])
         nc.tensor.transpose(g_turned[:], g_rows[:], ident[:])
-        g_cols = sb.tile([P, 2 * PACK], F32, name="g_cols")
-        nc.scalar.copy(g_cols[:], g_turned[:, : 2 * PACK])
-
-        def pick_scales(offsets, name):
-            picked = sb.tile([P, S], U8, name=name + "_picked", align_bytes=64)
-            nc.vector.tensor_copy(picked[:], scale_table[:].indirect(offsets[:]))
-            dealt = sb.tile([P, PACK * P], U8, name=name, align_bytes=64)
-            nc.vector.tensor_copy(
-                dealt[:].bitcast(I32).rearrange("p (t b e) -> p b t e", t=PACK, e=RUN // 4),
-                picked[:].bitcast(I32).rearrange("p (b t e) -> p b t e", t=PACK, e=RUN // 4),
-            )
-            return dealt
+        gi_cols = sb.tile([P, PACK], F32, name="gi_cols", tag="gi_cols", align_bytes=64)
+        gt_cols = sb.tile([P, PACK], F32, name="gt_cols")
+        nc.scalar.copy(gi_cols[:], g_turned[:, :PACK])
+        nc.scalar.copy(gt_cols[:], g_turned[:, PACK : 2 * PACK])
 
         def pick_words(offsets, name, tag):
             dealt = sb.tile([P, PACK * P], U32, name=name, tag=tag, align_bytes=64)
@@ -97,94 +89,138 @@ def tile_picked_momdiff_square_p_kernel(tc, x_words, x_scales, wa, wb, gt, gi, o
             )
             return dealt
 
-        def quantize_weight_half(raw, name, tag):
-            grouped = sb.tile([P, HALF, PACK], BF16, name=name + "_grouped", tag=tag, align_bytes=64)
-            nc.scalar.copy(side_by_side(grouped[:]), by_rows(raw[:]))
+        def quantized(grouped, name):
             codes = sb.tile([P, HALF], U32, name=name + "_codes", tag=name + "_codes", align_bytes=64)
             scales = sb.tile([P, HALF], U8, name=name + "_scales", align_bytes=64)
             quantize(nc, codes[:], scales[:], grouped[:])
             return codes, scales
 
-        xb_scales = pick_scales(two_sb, "xb_scales")
-        xa_scales = pick_scales(offs_sb, "xa_scales")
-        xb_words = pick_words(two_sb, "xb_words", "xb_words")
+        def grouped_tile(name, tag):
+            return sb.tile([P, HALF, PACK], BF16, name=name, tag=tag, align_bytes=64)
 
-        wbq = [quantize_weight_half(wb_raw[h], "wb%d" % h, "wb%d_grouped" % h) for h in range(2)]
-        window = [sb.tile([P, N], F32, name="window%d" % t) for t in range(PACK)]
+        def mx_pass(psum, stationary, rows, moving, cols, start=True, stop=True):
+            nc.tensor.matmul_mx(
+                out=psum, lhsT=stationary[0][:, rows].bitcast(FP8X4), lhsT_scale=stationary[1][:, rows],
+                rhs=moving[0][:, cols].bitcast(FP8X4), rhs_scale=moving[1][:, cols], start=start, stop=stop,
+            )
+
+        def block(i):
+            return slice(i * P, (i + 1) * P)
+
+        def half(h):
+            return slice(h * HALF, (h + 1) * HALF)
+
+        picked_scales = sb.tile([P, 2 * S], U8, name="picked_scales", align_bytes=64)
+        for i, offsets in enumerate((two_sb, offs_sb)):
+            nc.vector.tensor_copy(picked_scales[:, i * S : (i + 1) * S], scale_table[:].indirect(offsets[:]))
+        dealt_scales = sb.tile([P, 2 * S], U8, name="dealt_scales", align_bytes=64)
+        nc.vector.tensor_copy(
+            dealt_scales[:].bitcast(I32).rearrange("p (i t b e) -> p i b t e", i=2, t=PACK, e=RUN // 4),
+            picked_scales[:].bitcast(I32).rearrange("p (i b t e) -> p i b t e", i=2, t=PACK, e=RUN // 4),
+        )
+        xa = (pick_words(offs_sb, "xa_words", "xa_words"), dealt_scales[:, S:])
+        xb = (pick_words(two_sb, "xb_words", "xb_words"), dealt_scales[:, :S])
+
+        wa_grouped0 = grouped_tile("wa_grouped0", "wa_grouped0")
+        nc.scalar.copy(side_by_side(wa_grouped0[:]), by_rows(wa_raw[0][:]))
+        waq = [quantized(wa_grouped0, "wa0")]
+
+        wb_grouped = [grouped_tile("wb_grouped%d" % h, "wb_grouped%d" % h) for h in range(2)]
+        wbq = (
+            sb.tile([P, N], U32, name="wb_codes", tag="wb_codes", align_bytes=64),
+            sb.tile([P, N], U8, name="wb_scales", align_bytes=64),
+        )
         for h in range(2):
-            codes, scales = wbq[h]
-            for t in range(PACK):
-                rows = slice(t * P, (t + 1) * P)
-                b_ps = bank(PACK * h + t, [P, HALF])
-                nc.tensor.matmul_mx(
-                    out=b_ps[:], lhsT=xb_words[:, rows].bitcast(FP8X4), lhsT_scale=xb_scales[:, rows],
-                    rhs=codes[:].bitcast(FP8X4), rhs_scale=scales[:], start=True, stop=True,
-                )
-                nc.scalar.activation(window[t][:, h * HALF : (h + 1) * HALF], b_ps[:], ACT.Copy, scale=g_cols[:, t : t + 1])
+            nc.scalar.copy(side_by_side(wb_grouped[h][:]), by_rows(wb_raw[h][:]))
+            quantize(nc, wbq[0][:, half(h)], wbq[1][:, half(h)], wb_grouped[h][:])
 
-        xa_words = pick_words(offs_sb, "xa_words", "xa_words")
+        window = [sb.tile([P, N], F32, name="window%d" % t, tag="window%d" % t, align_bytes=64) for t in range(PACK)]
+        b_half = [[bank(2 * h + t, [P, HALF]) for t in range(2)] for h in range(2)]
+        b_whole = [bank(4 + t, [P, N]) for t in range(2)]
+        for h in range(2):
+            for t in range(2):
+                mx_pass(b_half[h][t][:], xb, block(t), wbq, half(h))
+        for t in range(2, PACK):
+            mx_pass(b_whole[t - 2][:], xb, block(t), wbq, slice(0, N))
+        for t in range(2):
+            for h in range(2):
+                nc.scalar.activation(window[t][:, half(h)], b_half[h][t][:], ACT.Copy, scale=gi_cols[:, t : t + 1])
+        for t in range(2, PACK):
+            nc.scalar.activation(window[t][:], b_whole[t - 2][:], ACT.Copy, scale=gi_cols[:, t : t + 1])
 
-        z2_rows = sb.tile([P, PACK, N], F32, name="z2_rows")
+        z2_rows = sb.tile([P, PACK, N], F32, name="z2_rows", tag="z2_rows", align_bytes=64)
         for t in range(PACK):
             nc.sync.dma_start(z2_rows[:, t, :], window[t][:])
 
-        z3_rows = [sb.tile([P, PACK, HALF], BF16, name="z3_rows%d" % h) for h in range(2)]
-        for h in range(2):
+        wa_grouped1 = grouped_tile("wa_grouped1", "wb_codes")
+        nc.scalar.copy(side_by_side(wa_grouped1[:]), by_rows(wa_raw[1][:]))
+
+        def fetch_half(h, tag):
+            rows = sb.tile([P, PACK, HALF], BF16, name="z3_rows%d" % h, tag=tag, align_bytes=64)
             for t in range(PACK):
-                nc.vector.tensor_copy(z3_rows[h][:, t, :], window[t][:].indirect(fl_sb[:, 16 * h : 16 * (h + 1)]))
-
-        waq = [quantize_weight_half(wa_raw[h], "wa%d" % h, ("xb_words", "wb1_codes")[h]) for h in range(2)]
-
-        zq = []
-        for h in range(2):
-            codes, scales = waq[h]
-            grouped = sb.tile([P, HALF, PACK], BF16, name="z_grouped%d" % h, align_bytes=64)
-            for u in range(2):
-                cols = slice(u * P, (u + 1) * P)
-                a_ps = bank(2 * h + u, [P, PACK, P])
-                for t in range(PACK):
-                    rows = slice(t * P, (t + 1) * P)
-                    nc.tensor.matmul_mx(
-                        out=a_ps[:, t, :], lhsT=xa_words[:, rows].bitcast(FP8X4), lhsT_scale=xa_scales[:, rows],
-                        rhs=codes[:, cols].bitcast(FP8X4), rhs_scale=scales[:, cols], start=True, stop=True,
-                    )
-                nc.vector.tensor_tensor(
-                    grouped[:, cols, :], a_ps[:].rearrange("p t c -> p c t"),
-                    g_cols[:, PACK:].unsqueeze(1).to_broadcast([P, P, PACK]), ALU.mult,
-                )
-            z_codes = sb.tile([P, HALF], U32, name="z_codes%d" % h, align_bytes=64)
-            z_scales = sb.tile([P, HALF], U8, name="z_scales%d" % h, align_bytes=64)
-            quantize(nc, z_codes[:], z_scales[:], grouped[:])
-            zq.append((z_codes, z_scales))
-
-        def quantized(grouped, name):
-            codes = sb.tile([P, HALF], U32, name=name + "_codes", align_bytes=64)
-            scales = sb.tile([P, HALF], U8, name=name + "_scales", align_bytes=64)
-            quantize(nc, codes[:], scales[:], grouped[:])
-            return codes, scales
+                nc.vector.tensor_copy(rows[:, t, :], window[t][:].indirect(fl_sb[:, 16 * h : 16 * (h + 1)]))
+            return rows
 
         def z2_half(h):
-            grouped = sb.tile([P, HALF, PACK], BF16, name="z2_grouped%d" % h, align_bytes=64)
-            nc.scalar.activation(side_by_side(grouped[:]), by_rows(z2_rows[:, :, h * HALF : (h + 1) * HALF]), ACT.Copy, scale=-1.0)
-            return quantized(grouped, "z2_%d" % h)
+            grouped = grouped_tile("z2_grouped%d" % h, "z2_grouped%d" % h)
+            nc.scalar.activation(side_by_side(grouped[:]), by_rows(z2_rows[:, :, half(h)]), ACT.Copy, scale=-1.0)
+            return grouped
 
         def z3_half(h):
-            grouped = sb.tile([P, HALF, PACK], BF16, name="z3_grouped%d" % h, align_bytes=64)
+            grouped = grouped_tile("z3_grouped%d" % h, ("z3_grouped0", "z2_rows")[h])
             nc.scalar.copy(side_by_side(grouped[:]), by_rows(z3_rows[h][:]))
-            return quantized(grouped, "z3_%d" % h)
+            return grouped
 
-        moving = [(z3_half(0), z2_half(0)), (z2_half(1), z3_half(1))]
+        def moments(zqs, movings, banks):
+            sums = [bank(b, [P, HALF]) for b in banks]
+            for step, moving in enumerate(movings):
+                for i, total in enumerate(sums):
+                    mx_pass(total[:], zqs[i // 2], block(i % 2), moving, slice(0, HALF), start=step == 0, stop=step == 1)
+            return sums
+
+        def finish(total, result, m, h, on_vector=False):
+            if on_vector:
+                scaled = sb.tile([P, HALF], F32, name="scaled%d" % h, tag=("z2_rows", "scaled1")[h], align_bytes=64)
+                nc.vector.tensor_scalar_mul(scaled[:], total[:], 0.03125)
+                nc.vector.tensor_tensor(result, scaled[:], scaled[:], ALU.mult)
+            else:
+                nc.scalar.activation(result, total[:], ACT.Square, scale=0.03125)
+            nc.sync.dma_start(out[block(m), half(h)], result)
+
+        def z_block(grouped, m, b):
+            a_ps = bank(b, [P, PACK, P])
+            for t in range(PACK):
+                mx_pass(a_ps[:, t, :], xa, block(t), waq[m // 2], block(m % 2))
+            nc.vector.tensor_tensor(
+                grouped, a_ps[:].rearrange("p t c -> p c t"),
+                gt_cols[:].unsqueeze(1).to_broadcast([P, P, PACK]), ALU.mult,
+            )
+
+        z3_rows = [fetch_half(0, "z3_rows0")]
+        z_first = [sb.tile([P, P, PACK], BF16, name="z_first%d" % m, tag="wb_grouped%d" % m, align_bytes=64) for m in range(2)]
+        zq0 = (
+            sb.tile([P, HALF], U32, name="z0_codes", tag="gi_cols", align_bytes=64),
+            sb.tile([P, HALF], U8, name="z0_scales", align_bytes=64),
+        )
+        for m in range(2):
+            z_block(z_first[m][:], m, 6 + m)
+        for m in range(2):
+            quantize(nc, zq0[0][:, block(m)], zq0[1][:, block(m)], z_first[m][:])
+        waq.append(quantized(wa_grouped1, "wa1"))
+        z3_rows.append(fetch_half(1, "wb_codes"))
+        z3q0 = quantized(z3_half(0), "z3_0")
+        z2q = [quantized(z2_half(0), "z2_0")]
+        z_grouped1 = grouped_tile("z_grouped1", "z2_grouped0")
+        for u in range(2):
+            z_block(z_grouped1[:, block(u), :], 2 + u, u)
+        z2q.append(quantized(z2_half(1), "z2_1"))
+        zq = [zq0, quantized(z_grouped1, "z1")]
+        z3q1 = quantized(z3_half(1), "z3_1")
+        sums = [
+            moments(zq, (z3q0, z2q[0]), (4, 5, 6, 7)),
+            moments(zq, (z2q[1], z3q1), (2, 3, 0, 1)),
+        ]
         for h in range(2):
-            m_ps = [bank(PACK * (1 - h) + m, [P, HALF]) for m in range(H // P)]
-            for step, (codes, scales) in enumerate(moving[h]):
-                for m in range(H // P):
-                    z_codes, z_scales = zq[m // 2]
-                    rows = slice((m % 2) * P, (m % 2 + 1) * P)
-                    nc.tensor.matmul_mx(
-                        out=m_ps[m][:], lhsT=z_codes[:, rows].bitcast(FP8X4), lhsT_scale=z_scales[:, rows],
-                        rhs=codes[:].bitcast(FP8X4), rhs_scale=scales[:], start=step == 0, stop=step == 1,
-                    )
+            results = sb.tile([P, H // P, HALF], F32, name="results%d" % h, tag=("wb_codes", "results1")[h], align_bytes=64)
             for m in range(H // P):
-                result = sb.tile([P, HALF], F32, name="result%d_%d" % (h, m))
-                nc.scalar.activation(result[:], m_ps[m][:], ACT.Square, scale=0.03125)
-                nc.sync.dma_start(out[m * P : (m + 1) * P, h * HALF : (h + 1) * HALF], result[:])
+                finish(sums[h][m], results[:, m, :], m, h, on_vector=(h, m) in ((0, 3), (1, 0)))

@@ -51,7 +51,7 @@ def tile_picked_momdiff_square_p_kernel(tc, x_words, x_scales, wa, wb, gt, gi, o
         fl_sb = sb.tile([P, N // 16], U16, name="fl_sb")
         nc.sync.dma_start(two_sb[:], two)
         for q in range(4):
-            (nc.scalar, nc.sync)[q % 2].dma_start(scale_table[32 * q : 32 * q + 4, :].bitcast(I32), x_scales[0, 4 * q : 4 * q + 4, :].bitcast(I32))
+            nc.sync.dma_start(scale_table[32 * q : 32 * q + 4, :].bitcast(I32), x_scales[0, 4 * q : 4 * q + 4, :].bitcast(I32))
         nc.sync.dma_start(offs_sb[:], offs)
         word_table = sb.tile([P, T], I32, name="word_table", align_bytes=64)
         nc.sync.dma_start(word_table[:], x_words[0].rearrange("p c r -> p (c r)").bitcast(I32))

@@ -167,8 +167,8 @@ def tile_picked_momdiff_square_p_kernel(tc, x_words, x_scales, wa, wb, gt, gi, o
             return grouped
 
         def z3_half(h):
-            grouped = grouped_tile("z3_grouped%d" % h, ("z3_grouped0", "z2_rows")[h])
-            nc.scalar.copy(side_by_side(grouped[:]), by_rows(z3_rows[h][:]))
+            grouped = grouped_tile("z3_grouped%d" % h, ("z3_grouped0", "z2_grouped0")[h])
+            (nc.scalar.copy, nc.vector.tensor_copy)[h](side_by_side(grouped[:]), by_rows(z3_rows[h][:]))
             return grouped
 
         def moments(zqs, movings, banks):
@@ -180,7 +180,7 @@ def tile_picked_momdiff_square_p_kernel(tc, x_words, x_scales, wa, wb, gt, gi, o
 
         def finish(total, result, m, h, on_vector=False):
             if on_vector:
-                scaled = sb.tile([P, HALF], F32, name="scaled%d" % h, tag=("z2_rows", "scaled1")[h], align_bytes=64)
+                scaled = sb.tile([P, HALF], F32, name="scaled%d" % h, tag=("z2_grouped0", "scaled1")[h], align_bytes=64)
                 nc.vector.tensor_scalar_mul(scaled[:], total[:], 0.03125)
                 nc.vector.tensor_tensor(result, scaled[:], scaled[:], ALU.mult)
             else:
@@ -207,20 +207,25 @@ def tile_picked_momdiff_square_p_kernel(tc, x_words, x_scales, wa, wb, gt, gi, o
         for m in range(2):
             quantize(nc, zq0[0][:, block(m)], zq0[1][:, block(m)], z_first[m][:])
         waq.append(quantized(wa_grouped1, "wa1"))
+        z_rows1 = sb.tile([P, PACK, HALF], BF16, name="z_rows1", align_bytes=64)
+        for t in range(PACK):
+            a_ps = bank(t, [P, HALF])
+            mx_pass(a_ps[:], xa, block(t), waq[1], slice(0, HALF))
+            nc.scalar.activation(z_rows1[:, t, :], a_ps[:], ACT.Copy, scale=gt_cols[:, t : t + 1])
         z3_rows.append(fetch_half(1, "wb_codes"))
+        z_grouped1 = grouped_tile("z_grouped1", "window0")
+        nc.vector.tensor_copy(side_by_side(z_grouped1[:]), by_rows(z_rows1[:]))
         z3q0 = quantized(z3_half(0), "z3_0")
-        z2q = [quantized(z2_half(0), "z2_0")]
-        z_grouped1 = grouped_tile("z_grouped1", "z2_grouped0")
-        for u in range(2):
-            z_block(z_grouped1[:, block(u), :], 2 + u, u)
-        z2q.append(quantized(z2_half(1), "z2_1"))
         zq = [zq0, quantized(z_grouped1, "z1")]
-        z3q1 = quantized(z3_half(1), "z3_1")
+        z2q = [quantized(z2_half(0), "z2_0")]
+        z3_grouped1 = z3_half(1)
+        z2q.append(quantized(z2_half(1), "z2_1"))
+        z3q1 = quantized(z3_grouped1, "z3_1")
         sums = [
             moments(zq, (z3q0, z2q[0]), (4, 5, 6, 7)),
-            moments(zq, (z2q[1], z3q1), (2, 3, 0, 1)),
+            moments(zq, (z2q[1], z3q1), (0, 1, 2, 3)),
         ]
         for h in range(2):
-            results = sb.tile([P, H // P, HALF], F32, name="results%d" % h, tag=("wb_codes", "results1")[h], align_bytes=64)
+            results = sb.tile([P, H // P, HALF], F32, name="results%d" % h, tag=("z2_rows", "results1")[h], align_bytes=64)
             for m in range(H // P):
-                finish(sums[h][m], results[:, m, :], m, h, on_vector=(h, m) in ((0, 3), (1, 0)))
+                finish(sums[h][m], results[:, m, :], m, h, on_vector=(h, m) in ((0, 3), (1, 1)))

from contextlib import ExitStack

import concourse.mybir as mybir
from concourse.masks import make_identity

K, T, S, N, H = 512, 2048, 512, 512, 512
FLOPS = 4 * 2 * 512 * 512 * 512

F32 = mybir.dt.float32
BF16 = mybir.dt.bfloat16
I32 = mybir.dt.int32
U32 = mybir.dt.uint32
U16 = mybir.dt.uint16
U8 = mybir.dt.uint8
FP8X4 = mybir.dt.float8_e4m3fn_x4
ACT = mybir.ActivationFunctionType
ALU = mybir.AluOpType

P = 128
PACK = 4
RUN = 8
HALF = 256
LINE = 4


def side_by_side(grouped):
    return grouped.rearrange("p (c i) t -> p c t i", i=LINE)


def by_rows(rows):
    return rows.rearrange("p t (c i) -> p c t i", i=LINE)


def quantize(nc, codes, scales, grouped):
    nc.vector.quantize_mx(out=codes.bitcast(FP8X4), scales=scales, in_=grouped.rearrange("p c t -> p (c t)"))


def tile_picked_momdiff_square_p_kernel(tc, x_words, x_scales, wa, wb, gt, gi, offs, two, fl, out):
    nc = tc.nc
    with ExitStack() as ctx:
        sb = ctx.enter_context(tc.tile_pool(name="sb", bufs=1))
        ps = ctx.enter_context(tc.psum_pool(name="ps", bufs=1))

        def bank(b, shape):
            return ps.tile(shape, F32, name="bank%d" % b, tag="bank%d" % b)

        scale_table = sb.tile([P, T], U8, name="scale_table", align_bytes=64)
        nc.gpsimd.memset(scale_table[:].bitcast(I32), 0)
        two_sb = sb.tile([P, S // 16], U16, name="two_sb")
        offs_sb = sb.tile([P, S // 16], U16, name="offs_sb")
        fl_sb = sb.tile([P, N // 16], U16, name="fl_sb")
        nc.sync.dma_start(two_sb[:], two)
        for q in range(4):
            nc.sync.dma_start(scale_table[32 * q : 32 * q + 4, :].bitcast(I32), x_scales[0, 4 * q : 4 * q + 4, :].bitcast(I32))
        nc.sync.dma_start(offs_sb[:], offs)
        word_table = sb.tile([P, T], I32, name="word_table", align_bytes=64)
        nc.sync.dma_start(word_table[:], x_words[0].rearrange("p c r -> p (c r)").bitcast(I32))

        def load_weight_half(w, h, name):
            raw = sb.tile([P, PACK, HALF], F32, name=name)
            nc.sync.dma_start(raw[:], w.rearrange("(p j) n -> p j n", j=PACK)[:, :, h * HALF : (h + 1) * HALF])
            return raw

        g_rows = sb.tile([P, P], F32, name="g_rows")
        nc.gpsimd.memset(g_rows[:], 0.0)
        for first, g in ((0, gi), (PACK, gt)):
            nc.sync.dma_start(
                g_rows[first : first + PACK, :].rearrange("t (b e) -> t b e", e=RUN),
                g.rearrange("(b t e) o -> t b (e o)", t=PACK, e=RUN),
            )
        wa_raw = [load_weight_half(wa, 0, "wa_raw0")]
        wb_raw = [load_weight_half(wb, h, "wb_raw%d" % h) for h in range(2)]
        nc.sync.dma_start(fl_sb[:], fl)
        wa_raw.append(load_weight_half(wa, 1, "wa_raw1"))
        ident = sb.tile([P, P], F32, name="ident")
        make_identity(nc, ident[:])
        g_turned = bank(7, [P, P])
        nc.tensor.transpose(g_turned[:], g_rows[:], ident[:])
        gi_cols = sb.tile([P, PACK], F32, name="gi_cols", tag="gi_cols", align_bytes=64)
        gt_cols = sb.tile([P, PACK], F32, name="gt_cols")
        nc.scalar.copy(gi_cols[:], g_turned[:, :PACK])
        nc.scalar.copy(gt_cols[:], g_turned[:, PACK : 2 * PACK])

        def pick_words(offsets, name, tag):
            dealt = sb.tile([P, PACK * P], U32, name=name, tag=tag, align_bytes=64)
            nc.vector.tensor_copy(
                dealt[:].rearrange("p (t b e) -> p b t e", t=PACK, e=RUN),
                word_table[:].bitcast(U32).indirect(offsets[:]),
            )
            return dealt

        def quantized(grouped, name):
            codes = sb.tile([P, HALF], U32, name=name + "_codes", tag=name + "_codes", align_bytes=64)
            scales = sb.tile([P, HALF], U8, name=name + "_scales", align_bytes=64)
            quantize(nc, codes[:], scales[:], grouped[:])
            return codes, scales

        def grouped_tile(name, tag):
            return sb.tile([P, HALF, PACK], BF16, name=name, tag=tag, align_bytes=64)

        def mx_pass(psum, stationary, rows, moving, cols, start=True, stop=True):
            nc.tensor.matmul_mx(
                out=psum, lhsT=stationary[0][:, rows].bitcast(FP8X4), lhsT_scale=stationary[1][:, rows],
                rhs=moving[0][:, cols].bitcast(FP8X4), rhs_scale=moving[1][:, cols], start=start, stop=stop,
            )

        def block(i):
            return slice(i * P, (i + 1) * P)

        def half(h):
            return slice(h * HALF, (h + 1) * HALF)

        picked_scales = sb.tile([P, 2 * S], U8, name="picked_scales", align_bytes=64)
        for i, offsets in enumerate((two_sb, offs_sb)):
            nc.vector.tensor_copy(picked_scales[:, i * S : (i + 1) * S], scale_table[:].indirect(offsets[:]))
        dealt_scales = sb.tile([P, 2 * S], U8, name="dealt_scales", align_bytes=64)
        nc.vector.tensor_copy(
            dealt_scales[:].bitcast(I32).rearrange("p (i t b e) -> p i b t e", i=2, t=PACK, e=RUN // 4),
            picked_scales[:].bitcast(I32).rearrange("p (i b t e) -> p i b t e", i=2, t=PACK, e=RUN // 4),
        )
        xa = (pick_words(offs_sb, "xa_words", "xa_words"), dealt_scales[:, S:])
        xb = (pick_words(two_sb, "xb_words", "xb_words"), dealt_scales[:, :S])

        wa_grouped0 = grouped_tile("wa_grouped0", "wa_grouped0")
        nc.scalar.copy(side_by_side(wa_grouped0[:]), by_rows(wa_raw[0][:]))
        waq = [quantized(wa_grouped0, "wa0")]

        wb_grouped = [grouped_tile("wb_grouped%d" % h, "wb_grouped%d" % h) for h in range(2)]
        wbq = (
            sb.tile([P, N], U32, name="wb_codes", tag="wb_codes", align_bytes=64),
            sb.tile([P, N], U8, name="wb_scales", align_bytes=64),
        )
        for h in range(2):
            nc.scalar.copy(side_by_side(wb_grouped[h][:]), by_rows(wb_raw[h][:]))
            quantize(nc, wbq[0][:, half(h)], wbq[1][:, half(h)], wb_grouped[h][:])

        window = [sb.tile([P, N], F32, name="window%d" % t, tag="window%d" % t, align_bytes=64) for t in range(PACK)]
        b_half = [[bank(2 * h + t, [P, HALF]) for t in range(2)] for h in range(2)]
        b_whole = [bank(4 + t, [P, N]) for t in range(2)]
        for h in range(2):
            for t in range(2):
                mx_pass(b_half[h][t][:], xb, block(t), wbq, half(h))
        for t in range(2, PACK):
            mx_pass(b_whole[t - 2][:], xb, block(t), wbq, slice(0, N))
        for t in range(2):
            for h in range(2):
                nc.scalar.activation(window[t][:, half(h)], b_half[h][t][:], ACT.Copy, scale=gi_cols[:, t : t + 1])
        for t in range(2, PACK):
            nc.scalar.activation(window[t][:], b_whole[t - 2][:], ACT.Copy, scale=gi_cols[:, t : t + 1])

        z2_rows = sb.tile([P, PACK, N], F32, name="z2_rows", tag="z2_rows", align_bytes=64)
        for t in range(PACK):
            nc.sync.dma_start(z2_rows[:, t, :], window[t][:])

        wa_grouped1 = grouped_tile("wa_grouped1", "wb_codes")
        nc.scalar.copy(side_by_side(wa_grouped1[:]), by_rows(wa_raw[1][:]))

        def fetch_half(h, tag):
            rows = sb.tile([P, PACK, HALF], BF16, name="z3_rows%d" % h, tag=tag, align_bytes=64)
            for t in range(PACK):
                nc.vector.tensor_copy(rows[:, t, :], window[t][:].indirect(fl_sb[:, 16 * h : 16 * (h + 1)]))
            return rows

        def z2_half(h):
            grouped = grouped_tile("z2_grouped%d" % h, "z2_grouped%d" % h)
            nc.scalar.activation(side_by_side(grouped[:]), by_rows(z2_rows[:, :, half(h)]), ACT.Copy, scale=-1.0)
            return grouped

        def z3_half(h):
            grouped = grouped_tile("z3_grouped%d" % h, ("z3_grouped0", "z2_grouped0")[h])
            (nc.scalar.copy, nc.vector.tensor_copy)[h](side_by_side(grouped[:]), by_rows(z3_rows[h][:]))
            return grouped

        def moments(zqs, movings, banks):
            sums = [bank(b, [P, HALF]) for b in banks]
            for step, moving in enumerate(movings):
                for i, total in enumerate(sums):
                    mx_pass(total[:], zqs[i // 2], block(i % 2), moving, slice(0, HALF), start=step == 0, stop=step == 1)
            return sums

        def finish(total, result, m, h, on_vector=False):
            if on_vector:
                scaled = sb.tile([P, HALF], F32, name="scaled%d" % h, tag=("z2_grouped0", "scaled1")[h], align_bytes=64)
                nc.vector.tensor_scalar_mul(scaled[:], total[:], 0.03125)
                nc.vector.tensor_tensor(result, scaled[:], scaled[:], ALU.mult)
            else:
                nc.scalar.activation(result, total[:], ACT.Square, scale=0.03125)
            nc.sync.dma_start(out[block(m), half(h)], result)

        def z_block(grouped, m, b):
            a_ps = bank(b, [P, PACK, P])
            for t in range(PACK):
                mx_pass(a_ps[:, t, :], xa, block(t), waq[m // 2], block(m % 2))
            nc.vector.tensor_tensor(
                grouped, a_ps[:].rearrange("p t c -> p c t"),
                gt_cols[:].unsqueeze(1).to_broadcast([P, P, PACK]), ALU.mult,
            )

        z3_rows = [fetch_half(0, "z3_rows0")]
        z_first = [sb.tile([P, P, PACK], BF16, name="z_first%d" % m, tag="wb_grouped%d" % m, align_bytes=64) for m in range(2)]
        zq0 = (
            sb.tile([P, HALF], U32, name="z0_codes", tag="gi_cols", align_bytes=64),
            sb.tile([P, HALF], U8, name="z0_scales", align_bytes=64),
        )
        for m in range(2):
            z_block(z_first[m][:], m, 6 + m)
        for m in range(2):
            quantize(nc, zq0[0][:, block(m)], zq0[1][:, block(m)], z_first[m][:])
        waq.append(quantized(wa_grouped1, "wa1"))
        z_rows1 = sb.tile([P, PACK, HALF], BF16, name="z_rows1", align_bytes=64)
        for t in range(PACK):
            a_ps = bank(t, [P, HALF])
            mx_pass(a_ps[:], xa, block(t), waq[1], slice(0, HALF))
            nc.scalar.activation(z_rows1[:, t, :], a_ps[:], ACT.Copy, scale=gt_cols[:, t : t + 1])
        z3_rows.append(fetch_half(1, "wb_codes"))
        z_grouped1 = grouped_tile("z_grouped1", "window0")
        nc.vector.tensor_copy(side_by_side(z_grouped1[:]), by_rows(z_rows1[:]))
        z3q0 = quantized(z3_half(0), "z3_0")
        zq = [zq0, quantized(z_grouped1, "z1")]
        z2q = [quantized(z2_half(0), "z2_0")]
        z3_grouped1 = z3_half(1)
        z2q.append(quantized(z2_half(1), "z2_1"))
        z3q1 = quantized(z3_grouped1, "z3_1")
        sums = [
            moments(zq, (z3q0, z2q[0]), (4, 5, 6, 7)),
            moments(zq, (z2q[1], z3q1), (0, 1, 2, 3)),
        ]
        for h in range(2):
            results = sb.tile([P, H // P, HALF], F32, name="results%d" % h, tag=("z2_rows", "results1")[h], align_bytes=64)
            for m in range(H // P):
                finish(sums[h][m], results[:, m, :], m, h, on_vector=(h, m) in ((0, 3), (1, 1)))
